import numpy as np
import ml_dtypes

BF16 = ml_dtypes.bfloat16


def bf(x):
    return np.asarray(x, np.float32).astype(BF16)


def f32(x):
    return np.asarray(x, np.float32)


def f64(x):
    return np.asarray(x).astype(np.float64)


def striped(idx):
    return np.tile(idx.reshape(-1, 16).T, (8, 1))


S, K, M, N, E, Q, V, D = 512, 128, 256, 384, 4, 96, 128, 4


def setup_inputs():
    return {"base": bf(np.random.standard_normal((M, S))), "x": bf(np.random.standard_normal((K, N))), "w": bf(1.5 * np.random.standard_normal((E, K, M)) / np.sqrt(K)), "b": f32(0.5 * np.random.standard_normal((M, 1))), "offs": striped(np.random.permutation(S)[:N])}


def reference(base, x, w, b, offs):
    idx = offs[:16].T.reshape(-1)
    z = f64(base).copy()
    for e in range(E):
        z[:, idx[e * Q : (e + 1) * Q]] += f64(w)[e].T @ f64(x)[:, e * Q : (e + 1) * Q]
    z = np.maximum(z + f64(b), 0.0)
    return z.reshape(M, V, D).mean(axis=2)

@@ -1,0 +1,73 @@
+import concourse.mybir as mybir
+from concourse.masks import make_identity
+
+P = 128
+M = 256
+S = 512
+N = 384
+E = 4
+D = 4
+BLOCKS = M // P
+PIECE = N // E
+OFFSET_COLUMNS = PIECE // 16
+
+FLOPS = 2 * P * M * N
+
+BF16, F32, U16 = mybir.dt.bfloat16, mybir.dt.float32, mybir.dt.uint16
+
+
+def tile_rows_unpool_mean_relu_kernel(tc, base, x, w, b, offs, out):
+    nc = tc.nc
+    with (
+        tc.tile_pool(name="held", bufs=1) as held,
+        tc.psum_pool(name="psum", bufs=1) as psum,
+    ):
+        base_tile = held.tile([P, BLOCKS, S], BF16)
+        offsets = held.tile([P, N // 16], U16)
+        points = held.tile([P, N], BF16)
+        weights = held.tile([P, E, M], BF16)
+        bias = held.tile([P, BLOCKS], F32)
+        nc.sync.dma_start(base_tile[:], base.rearrange("(a p) s -> p a s", p=P))
+        nc.sync.dma_start(offsets[:], offs)
+        nc.sync.dma_start(points[:], x)
+        nc.sync.dma_start(weights[:], w.rearrange("e k m -> k e m"))
+        nc.scalar.dma_start(bias[:], b.rearrange("(a p) o -> p (a o)", p=P))
+
+        ident = held.tile([P, P], BF16)
+        make_identity(nc, ident[:])
+
+        bias_part = held.tile([P, BLOCKS], F32)
+        nc.vector.tensor_scalar_mul(bias_part[:], bias[:], 1.0 / D)
+
+        windows = [psum.tile([P, S], F32, name=f"window{a}") for a in range(BLOCKS)]
+        for a in range(BLOCKS):
+            nc.tensor.matmul(windows[a][:], ident[:], base_tile[:, a, :], start=True, stop=False)
+
+        for a in range(BLOCKS):
+            for e in range(E):
+                cells = offsets[:, e * OFFSET_COLUMNS : (e + 1) * OFFSET_COLUMNS]
+                nc.tensor.matmul(
+                    windows[a][:].indirect(cells),
+                    weights[:, e, a * P : (a + 1) * P],
+                    points[:, e * PIECE : (e + 1) * PIECE],
+                    start=False,
+                    stop=e == E - 1,
+                )
+
+        for a in range(BLOCKS):
+            active = held.tile([P, S], F32, name=f"active{a}")
+            nc.scalar.activation(
+                active[:],
+                windows[a][:],
+                mybir.ActivationFunctionType.Relu,
+                bias=bias_part[:, a : a + 1],
+                scale=1.0 / D,
+            )
+            pooled = held.tile([P, S // D], F32, name=f"pooled{a}")
+            nc.vector.tensor_reduce(
+                pooled[:],
+                active[:].rearrange("p (v d) -> p v d", d=D),
+                mybir.AxisListType.X,
+                mybir.AluOpType.add,
+            )
+            nc.sync.dma_start(out[a * P : (a + 1) * P, :], pooled[:])

@@ -10,6 +10,7 @@ D = 4
 BLOCKS = M // P
 PIECE = N // E
 OFFSET_COLUMNS = PIECE // 16
+WARM_UPS = 4
 
 FLOPS = 2 * P * M * N
 
@@ -35,6 +36,12 @@ def tile_rows_unpool_mean_relu_kernel(tc, base, x, w, b, offs, out):
 
         ident = held.tile([P, P], BF16)
         make_identity(nc, ident[:])
+
+        zeros = held.tile([P, S], BF16)
+        nc.vector.memset(zeros[:], 0.0)
+        spare = psum.tile([P, S], F32)
+        for warm_up in range(WARM_UPS):
+            nc.tensor.matmul(spare[:], zeros[:, :P], zeros[:], start=True, stop=True)
 
         bias_part = held.tile([P, BLOCKS], F32)
         nc.vector.tensor_scalar_mul(bias_part[:], bias[:], 1.0 / D)

@@ -7,10 +7,11 @@ S = 512
 N = 384
 E = 4
 D = 4
+V = S // D
 BLOCKS = M // P
 PIECE = N // E
 OFFSET_COLUMNS = PIECE // 16
-WARM_UPS = 4
+WARM_UPS = 8
 
 FLOPS = 2 * P * M * N
 
@@ -34,14 +35,17 @@ def tile_rows_unpool_mean_relu_kernel(tc, base, x, w, b, offs, out):
         nc.sync.dma_start(weights[:], w.rearrange("e k m -> k e m"))
         nc.scalar.dma_start(bias[:], b.rearrange("(a p) o -> p (a o)", p=P))
 
+        zeros = held.tile([P, 2 * P], BF16)
+        nc.gpsimd.memset(zeros[:], 0.0)
+        spare = psum.tile([P, 2 * P], F32)
+        for warm_up in range(WARM_UPS):
+            nc.tensor.matmul(spare[:], zeros[:, :P], zeros[:], start=True, stop=True)
+
         ident = held.tile([P, P], BF16)
         make_identity(nc, ident[:])
 
-        zeros = held.tile([P, S], BF16)
-        nc.vector.memset(zeros[:], 0.0)
-        spare = psum.tile([P, S], F32)
-        for warm_up in range(WARM_UPS):
-            nc.tensor.matmul(spare[:], zeros[:, :P], zeros[:], start=True, stop=True)
+        table_load = held.tile([P, 1], F32)
+        nc.scalar.activation(table_load[:], zeros[:, :1], mybir.ActivationFunctionType.Relu)
 
         bias_part = held.tile([P, BLOCKS], F32)
         nc.vector.tensor_scalar_mul(bias_part[:], bias[:], 1.0 / D)
@@ -62,19 +66,20 @@ def tile_rows_unpool_mean_relu_kernel(tc, base, x, w, b, offs, out):
                 )
 
         for a in range(BLOCKS):
-            active = held.tile([P, S], F32, name=f"active{a}")
-            nc.scalar.activation(
-                active[:],
-                windows[a][:],
-                mybir.ActivationFunctionType.Relu,
-                bias=bias_part[:, a : a + 1],
-                scale=1.0 / D,
-            )
-            pooled = held.tile([P, S // D], F32, name=f"pooled{a}")
-            nc.vector.tensor_reduce(
-                pooled[:],
-                active[:].rearrange("p (v d) -> p v d", d=D),
-                mybir.AxisListType.X,
-                mybir.AluOpType.add,
-            )
+            pooled = held.tile([P, V], F32, name=f"pooled{a}")
+            for h in range(2):
+                active = held.tile([P, S // 2], F32, name=f"active{a}{h}")
+                nc.scalar.activation(
+                    active[:],
+                    windows[a][:, h * S // 2 : (h + 1) * S // 2],
+                    mybir.ActivationFunctionType.Relu,
+                    bias=bias_part[:, a : a + 1],
+                    scale=1.0 / D,
+                )
+                nc.vector.tensor_reduce(
+                    pooled[:, h * V // 2 : (h + 1) * V // 2],
+                    active[:].rearrange("p (v d) -> p v d", d=D),
+                    mybir.AxisListType.X,
+                    mybir.AluOpType.add,
+                )
             nc.sync.dma_start(out[a * P : (a + 1) * P, :], pooled[:])

@@ -32,7 +32,8 @@ def tile_rows_unpool_mean_relu_kernel(tc, base, x, w, b, offs, out):
         nc.sync.dma_start(base_tile[:], base.rearrange("(a p) s -> p a s", p=P))
         nc.sync.dma_start(offsets[:], offs)
         nc.sync.dma_start(points[:], x)
-        nc.sync.dma_start(weights[:], w.rearrange("e k m -> k e m"))
+        for half in (slice(0, E // 2), slice(E // 2, E)):
+            nc.sync.dma_start(weights[:, half, :], w[half].rearrange("e k m -> k e m"))
         nc.scalar.dma_start(bias[:], b.rearrange("(a p) o -> p (a o)", p=P))
 
         zeros = held.tile([P, 2 * P], BF16)

import concourse.mybir as mybir
from concourse.masks import make_identity

P = 128
M = 256
S = 512
N = 384
E = 4
D = 4
V = S // D
BLOCKS = M // P
PIECE = N // E
OFFSET_COLUMNS = PIECE // 16
WARM_UPS = 8

FLOPS = 2 * P * M * N

BF16, F32, U16 = mybir.dt.bfloat16, mybir.dt.float32, mybir.dt.uint16


def tile_rows_unpool_mean_relu_kernel(tc, base, x, w, b, offs, out):
    nc = tc.nc
    with (
        tc.tile_pool(name="held", bufs=1) as held,
        tc.psum_pool(name="psum", bufs=1) as psum,
    ):
        base_tile = held.tile([P, BLOCKS, S], BF16)
        offsets = held.tile([P, N // 16], U16)
        points = held.tile([P, N], BF16)
        weights = held.tile([P, E, M], BF16)
        bias = held.tile([P, BLOCKS], F32)
        nc.sync.dma_start(base_tile[:], base.rearrange("(a p) s -> p a s", p=P))
        nc.sync.dma_start(offsets[:], offs)
        nc.sync.dma_start(points[:], x)
        for half in (slice(0, E // 2), slice(E // 2, E)):
            nc.sync.dma_start(weights[:, half, :], w[half].rearrange("e k m -> k e m"))
        nc.scalar.dma_start(bias[:], b.rearrange("(a p) o -> p (a o)", p=P))

        zeros = held.tile([P, 2 * P], BF16)
        nc.gpsimd.memset(zeros[:], 0.0)
        spare = psum.tile([P, 2 * P], F32)
        for warm_up in range(WARM_UPS):
            nc.tensor.matmul(spare[:], zeros[:, :P], zeros[:], start=True, stop=True)

        ident = held.tile([P, P], BF16)
        make_identity(nc, ident[:])

        table_load = held.tile([P, 1], F32)
        nc.scalar.activation(table_load[:], zeros[:, :1], mybir.ActivationFunctionType.Relu)

        bias_part = held.tile([P, BLOCKS], F32)
        nc.vector.tensor_scalar_mul(bias_part[:], bias[:], 1.0 / D)

        windows = [psum.tile([P, S], F32, name=f"window{a}") for a in range(BLOCKS)]
        for a in range(BLOCKS):
            nc.tensor.matmul(windows[a][:], ident[:], base_tile[:, a, :], start=True, stop=False)

        for a in range(BLOCKS):
            for e in range(E):
                cells = offsets[:, e * OFFSET_COLUMNS : (e + 1) * OFFSET_COLUMNS]
                nc.tensor.matmul(
                    windows[a][:].indirect(cells),
                    weights[:, e, a * P : (a + 1) * P],
                    points[:, e * PIECE : (e + 1) * PIECE],
                    start=False,
                    stop=e == E - 1,
                )

        for a in range(BLOCKS):
            pooled = held.tile([P, V], F32, name=f"pooled{a}")
            for h in range(2):
                active = held.tile([P, S // 2], F32, name=f"active{a}{h}")
                nc.scalar.activation(
                    active[:],
                    windows[a][:, h * S // 2 : (h + 1) * S // 2],
                    mybir.ActivationFunctionType.Relu,
                    bias=bias_part[:, a : a + 1],
                    scale=1.0 / D,
                )
                nc.vector.tensor_reduce(
                    pooled[:, h * V // 2 : (h + 1) * V // 2],
                    active[:].rearrange("p (v d) -> p v d", d=D),
                    mybir.AxisListType.X,
                    mybir.AluOpType.add,
                )
            nc.sync.dma_start(out[a * P : (a + 1) * P, :], pooled[:])
